import numpy as np
import ml_dtypes


def mxq(x, axis, fmt="e4m3"):
    dtype, down = {"e4m3": (ml_dtypes.float8_e4m3fn, 7), "e5m2": (ml_dtypes.float8_e5m2, 14)}[fmt]
    v = np.moveaxis(np.asarray(x, np.float32).astype(ml_dtypes.bfloat16).astype(np.float64), axis, -1)
    blocks = v.reshape(v.shape[:-1] + (-1, 32))
    amax = np.abs(blocks).max(-1, keepdims=True)
    byte = np.maximum(np.where(amax > 0, np.frexp(amax)[1] - 1 + 127, 0) - down, 1)
    scale = np.exp2(byte - 127.0)
    codes = (blocks / scale).astype(np.float32).astype(dtype).astype(np.float64)
    return np.moveaxis((codes * scale).reshape(v.shape), -1, axis)


WIDE = False


def mx_kscale(k):
    if not WIDE:
        return np.ones(k)
    levels = np.array([10, -10, 5, -5, 0])
    if k % 512:
        return np.exp2(np.random.permutation(np.resize(levels, k // 32))).repeat(32)
    a = np.empty((k // 512, 16))
    for p in range(k // 512):
        a[p, :8] = np.random.permutation(np.resize(levels, 8))
        for g in range(8):
            far = levels[np.abs(levels - a[p, g]) >= 10]
            a[p, g + 8] = far[np.random.randint(len(far))]
    return np.exp2(a.ravel()).repeat(32)


def f64(x):
    return np.asarray(x).astype(np.float64)


def striped(idx):
    return np.tile(idx.reshape(-1, 16).T, (8, 1)).astype(np.uint16)


def unstriped(offs):
    return offs[:16].T.reshape(-1).astype(np.int64)


def pack_weight(w):
    k, n = w.shape
    w = f64(np.asarray(w, np.float32).astype(ml_dtypes.bfloat16)).reshape(k // 32, 32, n)
    amax = np.abs(w).max(1)
    byte = np.clip(np.where(amax > 0, np.frexp(amax)[1] - 1 + 127 - 7, 1), 1, 254)
    scaled = (w * np.exp2(127.0 - byte)[:, None, :]).reshape(k, n).astype(np.float32)
    words = np.ascontiguousarray(scaled.reshape(k // 512, 128, 4, n).transpose(0, 1, 3, 2)).astype(ml_dtypes.float8_e4m3fn).view(np.uint8)
    return words, np.ascontiguousarray(byte.astype(np.uint8).reshape(k // 512, 16, n))


def unpack_weight(words, scales):
    g, p, n, _ = words.shape
    vals = np.ascontiguousarray(words).view(ml_dtypes.float8_e4m3fn).astype(np.float64) * np.repeat(np.exp2(scales.astype(np.float64) - 127.0), 8, axis=1)[..., None]
    return vals.transpose(0, 1, 3, 2).reshape(g * 512, n)


K, T, S, N = 512, 1024, 512, 256
P = 2 ** 7


def setup_inputs():
    n = np.random.standard_normal
    s = mx_kscale(K)[:, None]
    packed_xT = pack_weight(n((K, T)) * s)
    return {
        "x_words": packed_xT[0],
        "x_scales": packed_xT[1],
        "w1": (n((K, N)) / np.sqrt(K) / s).astype(np.float32),
        "w2": (n((K, N)) / np.sqrt(K) / s).astype(np.float32),
        "csd": (np.random.uniform(0.1, 0.6, (N, 1))).astype(np.float32),
        "wall": (np.tile(np.random.uniform(0.2, 1.0, S), (P, 1))).astype(np.float32),
        "offs": striped(np.random.permutation(T)[:S]),
        "east": striped(np.random.permutation(S)),
        "west": striped(np.random.permutation(S)),
        "north": striped(np.random.permutation(S)),
        "south": striped(np.random.permutation(S)),
    }


def reference(x_words, x_scales, w1, w2, csd, wall, offs, east, west, north, south):
    xq = unpack_weight(x_words, x_scales)[:, unstriped(offs)]
    uu = mxq(f64(w1), 0, "e4m3").T @ xq
    ux = 0.5 * (uu[:, unstriped(east)] - uu[:, unstriped(west)])
    vv = mxq(f64(w2), 0, "e4m3").T @ xq
    vy = 0.5 * (vv[:, unstriped(north)] - vv[:, unstriped(south)])
    uy = 0.5 * (uu[:, unstriped(north)] - uu[:, unstriped(south)])
    vx = 0.5 * (vv[:, unstriped(east)] - vv[:, unstriped(west)])
    sxy = 0.5 * (uy + vx)
    smag = np.sqrt(2.0 * ((ux) ** 2 + (vy) ** 2 + 2.0 * ((sxy) ** 2)) + 0.02)
    nut = (f64(csd) * smag) * f64(wall)[:1]
    rot = uy - vx
    return nut * ((smag) ** 2) - (0.2 * ((rot) ** 2))

@@ -1,0 +1,186 @@
+import math
+from contextlib import ExitStack
+
+import concourse.mybir as mybir
+from concourse.masks import make_identity
+
+F32 = mybir.dt.float32
+BF16 = mybir.dt.bfloat16
+I32 = mybir.dt.int32
+U32 = mybir.dt.uint32
+U16 = mybir.dt.uint16
+U8 = mybir.dt.uint8
+FP8X4 = mybir.dt.float8_e4m3fn_x4
+ACT = mybir.ActivationFunctionType
+ALU = mybir.AluOpType
+
+P = 128
+K, T, S, N = 512, 1024, 512, 256
+PACK = 4
+HALF = S // 2
+FLOPS = 2 * 2 * K * N * S
+PIECES = [(0, 0, 256), (0, 256, 512), (1, 0, 256), (1, 256, 512)]
+
+
+def tile_picked_yturbo_prod_p_kernel(
+    tc, x_words, x_scales, w1, w2, csd, wall, offs, east, west, north, south, out
+):
+    nc = tc.nc
+    with ExitStack() as ctx:
+        keep = ctx.enter_context(tc.tile_pool(name="keep", bufs=1))
+        work = ctx.enter_context(tc.tile_pool(name="work", bufs=3))
+        psum = ctx.enter_context(tc.psum_pool(name="psum", bufs=1))
+
+        lists = {}
+        for name in ("offs", "east", "west", "north", "south"):
+            lists[name] = keep.tile([P, S // 16], U16, name="list_" + name)
+        words_all = keep.tile([P, T], U32, name="words_all", align_bytes=64)
+        scales_all = keep.tile([P, T], U8, name="scales_all", align_bytes=64)
+        w_raw = [keep.tile([P, PACK, N], F32, name="w_raw%d" % f) for f in range(2)]
+        one = keep.tile([P, 1], F32, name="one")
+        floor_col = keep.tile([P, 1], F32, name="floor_col")
+        wall_cols = keep.tile([P, S // P], F32, name="wall_cols")
+        csd_cols = keep.tile([P, N // P], F32, name="csd_cols")
+        ident = keep.tile([P, P], F32, name="ident")
+
+        nc.vector.memset(scales_all[:].bitcast(I32), 0)
+        nc.vector.memset(one[:], 1.0)
+        nc.sync.dma_start(lists["offs"][:], offs)
+        nc.sync.dma_start(words_all[:].bitcast(I32), x_words[0].rearrange("p n t -> p (n t)").bitcast(I32))
+        for q in range(4):
+            nc.scalar.dma_start(
+                scales_all[32 * q : 32 * q + 4, :].bitcast(I32), x_scales[0, 4 * q : 4 * q + 4, :].bitcast(I32)
+            )
+        nc.sync.dma_start(w_raw[0][:], w1.rearrange("(p j) n -> p j n", j=PACK))
+        nc.sync.dma_start(w_raw[1][:], w2.rearrange("(p j) n -> p j n", j=PACK))
+        nc.sync.dma_start(lists["west"][:], west)
+        nc.sync.dma_start(lists["south"][:], south)
+        nc.sync.dma_start(lists["north"][:], north)
+        nc.sync.dma_start(lists["east"][:], east)
+        with nc.allow_non_contiguous_dma(reason="one factor a partition"):
+            nc.sync.dma_start(wall_cols[:], wall[0:1, :].rearrange("o (b p) -> p (o b)", p=P))
+            nc.sync.dma_start(csd_cols[:], csd.rearrange("(t p) o -> p (t o)", p=P))
+        nc.scalar.activation(floor_col[:], one[:], ACT.Sqrt, scale=0.02 * 0.02)
+        make_identity(nc, ident[:])
+
+        scales_picked = keep.tile([P, S], U8, name="scales_picked", align_bytes=64)
+        nc.vector.tensor_copy(scales_picked[:], scales_all[:].indirect(lists["offs"][:]))
+        words_picked = []
+        for h in range(2):
+            wp = keep.tile([P, HALF], U32, name="words_picked%d" % h, align_bytes=64)
+            nc.vector.tensor_copy(wp[:], words_all[:].indirect(lists["offs"][:, h * 16 : (h + 1) * 16]))
+            words_picked.append(wp)
+
+        codes = {}
+        planes = {}
+        fields = {}
+        for f, t in ((0, 0), (0, 1), (1, 0), (1, 1)):
+            grouped = keep.tile([P, P, PACK], BF16, name="grouped%d%d" % (f, t), align_bytes=64)
+            src = w_raw[f][:, :, t * P : (t + 1) * P].rearrange("p j (c i) -> p c j i", i=4)
+            dst = grouped[:].rearrange("p (c i) j -> p c j i", i=4)
+            if f == 0:
+                nc.scalar.copy(dst, src)
+            else:
+                nc.vector.tensor_copy(dst, src)
+            codes[f, t] = keep.tile([P, P], U32, name="codes%d%d" % (f, t), align_bytes=64)
+            planes[f, t] = keep.tile([P, P], U8, name="planes%d%d" % (f, t), align_bytes=64)
+            nc.vector.quantize_mx(
+                out=codes[f, t][:].bitcast(FP8X4),
+                scales=planes[f, t][:],
+                in_=grouped[:].rearrange("p c j -> p (c j)"),
+            )
+
+        for n, (f, t) in enumerate(((0, 0), (1, 0), (0, 1), (1, 1))):
+            fields[f, t] = keep.tile([P, S], F32, name="field%d%d" % (f, t))
+            for h in range(2):
+                bank = psum.tile([P, HALF], F32, name="mm%d%d%d" % (f, t, h), tag="bank%d" % ((2 * n + h) % 4))
+                nc.tensor.matmul_mx(
+                    out=bank[:],
+                    lhsT=codes[f, t][:].bitcast(FP8X4),
+                    lhsT_scale=planes[f, t][:],
+                    rhs=words_picked[h][:].bitcast(FP8X4),
+                    rhs_scale=scales_picked[:, h * HALF : (h + 1) * HALF],
+                    start=True,
+                    stop=True,
+                )
+                if h == 0:
+                    nc.scalar.copy(fields[f, t][:, h * HALF : (h + 1) * HALF], bank[:])
+                else:
+                    nc.vector.tensor_copy(fields[f, t][:, h * HALF : (h + 1) * HALF], bank[:])
+
+        state = {}
+
+        def differences(k):
+            t, j0, j1 = PIECES[k]
+            w = j1 - j0
+            u, v = fields[0, t], fields[1, t]
+
+            def at(field, name):
+                return field[:].indirect(lists[name][:, j0 // 16 : j1 // 16])
+
+            def fresh(name):
+                return work.tile([P, w], F32, name=name, tag=name)
+
+            u_s, u_w, v_s = fresh("u_s"), fresh("u_w"), fresh("v_s")
+            nc.scalar.activation(u_s[:], at(u, "south"), ACT.Copy)
+            nc.scalar.activation(u_w[:], at(u, "west"), ACT.Copy)
+            nc.scalar.activation(v_s[:], at(v, "south"), ACT.Copy)
+            a, b, c, x, p, q = (fresh(name) for name in ("a", "b", "c", "x", "p", "q"))
+            nc.vector.tensor_tensor(c[:], at(u, "north"), u_s[:], ALU.subtract)
+            nc.vector.tensor_tensor(a[:], at(u, "east"), u_w[:], ALU.subtract)
+            nc.vector.tensor_tensor(x[:], at(v, "west"), c[:], ALU.subtract)
+            nc.vector.tensor_tensor(b[:], at(v, "north"), v_s[:], ALU.subtract)
+            nc.vector.tensor_tensor(p[:], at(v, "east"), x[:], ALU.subtract)
+            nc.vector.scalar_tensor_tensor(q[:], c[:], 2.0, p[:], ALU.mult, ALU.subtract)
+            state[k] = (a, b, p, q)
+
+        def squares(k):
+            t, j0, j1 = PIECES[k]
+            w = j1 - j0
+            a, b, p, q = state[k]
+            sq = [work.tile([P, w], F32, name="sq%d" % i, tag="sq%d" % i) for i in range(4)]
+            nc.scalar.activation(sq[0][:], a[:], ACT.Square, scale=math.sqrt(0.5))
+            nc.scalar.activation(sq[1][:], b[:], ACT.Square, scale=math.sqrt(0.5))
+            nc.scalar.activation(sq[2][:], p[:], ACT.Square, scale=0.5)
+            nc.scalar.activation(sq[3][:], q[:], ACT.Square, scale=math.sqrt(0.05))
+            strain = psum.tile([P, w], F32, name="strain%d" % k, tag="strain%d" % (k % 2))
+            for blk in range(w // P):
+                cols = slice(blk * P, (blk + 1) * P)
+                terms = [floor_col[:].to_broadcast([P, P])] + [s[:, cols] for s in sq[:3]]
+                for i, term in enumerate(terms):
+                    nc.tensor.matmul(
+                        strain[:, cols], lhsT=term, rhs=ident[:], is_transpose=True, start=(i == 0), stop=(i == 3)
+                    )
+            state[k] = (strain, sq[3])
+
+        def finish(k):
+            t, j0, j1 = PIECES[k]
+            w = j1 - j0
+            strain, rot2 = state[k]
+            smag = work.tile([P, w], F32, name="smag", tag="smag")
+            nc.scalar.activation(smag[:], strain[:], ACT.Sqrt)
+            cube = work.tile([P, w], F32, name="cube", tag="cube")
+            back = psum.tile([P, w], F32, name="back%d" % k, tag="back%d" % (k % 2))
+            for blk in range(w // P):
+                cols = slice(blk * P, (blk + 1) * P)
+                jb = j0 // P + blk
+                nc.vector.scalar_tensor_tensor(
+                    cube[:, cols], strain[:, cols], wall_cols[:, jb : jb + 1], smag[:, cols], ALU.mult, ALU.mult
+                )
+            for blk in range(w // P):
+                cols = slice(blk * P, (blk + 1) * P)
+                nc.tensor.transpose(back[:, cols], cube[:, cols], ident[:])
+            result = work.tile([P, w], F32, name="result", tag="result")
+            nc.vector.scalar_tensor_tensor(
+                result[:], back[:], csd_cols[:, t : t + 1], rot2[:], ALU.mult, ALU.subtract
+            )
+            nc.sync.dma_start(out[t * P : (t + 1) * P, j0:j1], result[:])
+
+        count = len(PIECES)
+        for step in range(count + 2):
+            if step < count:
+                differences(step)
+            if 0 <= step - 1 < count:
+                squares(step - 1)
+            if 0 <= step - 2 < count:
+                finish(step - 2)

@@ -19,7 +19,6 @@ K, T, S, N = 512, 1024, 512, 256
 PACK = 4
 HALF = S // 2
 FLOPS = 2 * 2 * K * N * S
-PIECES = [(0, 0, 256), (0, 256, 512), (1, 0, 256), (1, 256, 512)]
 
 
 def tile_picked_yturbo_prod_p_kernel(
@@ -28,7 +27,6 @@ def tile_picked_yturbo_prod_p_kernel(
     nc = tc.nc
     with ExitStack() as ctx:
         keep = ctx.enter_context(tc.tile_pool(name="keep", bufs=1))
-        work = ctx.enter_context(tc.tile_pool(name="work", bufs=3))
         psum = ctx.enter_context(tc.psum_pool(name="psum", bufs=1))
 
         lists = {}
@@ -36,25 +34,28 @@ def tile_picked_yturbo_prod_p_kernel(
             lists[name] = keep.tile([P, S // 16], U16, name="list_" + name)
         words_all = keep.tile([P, T], U32, name="words_all", align_bytes=64)
         scales_all = keep.tile([P, T], U8, name="scales_all", align_bytes=64)
-        w_raw = [keep.tile([P, PACK, N], F32, name="w_raw%d" % f) for f in range(2)]
+        w1_raw = [keep.tile([P, PACK, P], F32, name="w1_raw%d" % t) for t in range(2)]
+        w2_raw = keep.tile([P, PACK, N], F32, name="w2_raw")
+        w_raw = {(0, 0): w1_raw[0][:], (0, 1): w1_raw[1][:], (1, 0): w2_raw[:, :, 0:P], (1, 1): w2_raw[:, :, P:N]}
         one = keep.tile([P, 1], F32, name="one")
         floor_col = keep.tile([P, 1], F32, name="floor_col")
         wall_cols = keep.tile([P, S // P], F32, name="wall_cols")
         csd_cols = keep.tile([P, N // P], F32, name="csd_cols")
         ident = keep.tile([P, P], F32, name="ident")
 
-        nc.vector.memset(scales_all[:].bitcast(I32), 0)
+        nc.gpsimd.memset(scales_all[:].bitcast(I32), 0)
         nc.vector.memset(one[:], 1.0)
         nc.sync.dma_start(lists["offs"][:], offs)
-        nc.sync.dma_start(words_all[:].bitcast(I32), x_words[0].rearrange("p n t -> p (n t)").bitcast(I32))
+        nc.sync.dma_start(lists["south"][:], south)
         for q in range(4):
-            nc.scalar.dma_start(
+            nc.sync.dma_start(
                 scales_all[32 * q : 32 * q + 4, :].bitcast(I32), x_scales[0, 4 * q : 4 * q + 4, :].bitcast(I32)
             )
-        nc.sync.dma_start(w_raw[0][:], w1.rearrange("(p j) n -> p j n", j=PACK))
-        nc.sync.dma_start(w_raw[1][:], w2.rearrange("(p j) n -> p j n", j=PACK))
+        nc.sync.dma_start(words_all[:].bitcast(I32), x_words[0].rearrange("p n t -> p (n t)").bitcast(I32))
+        nc.sync.dma_start(w1_raw[0][:], w1[:, 0:P].rearrange("(p j) n -> p j n", j=PACK))
+        nc.sync.dma_start(w2_raw[:], w2.rearrange("(p j) n -> p j n", j=PACK))
         nc.sync.dma_start(lists["west"][:], west)
-        nc.sync.dma_start(lists["south"][:], south)
+        nc.sync.dma_start(w1_raw[1][:], w1[:, P:N].rearrange("(p j) n -> p j n", j=PACK))
         nc.sync.dma_start(lists["north"][:], north)
         nc.sync.dma_start(lists["east"][:], east)
         with nc.allow_non_contiguous_dma(reason="one factor a partition"):
@@ -62,23 +63,27 @@ def tile_picked_yturbo_prod_p_kernel(
             nc.sync.dma_start(csd_cols[:], csd.rearrange("(t p) o -> p (t o)", p=P))
         nc.scalar.activation(floor_col[:], one[:], ACT.Sqrt, scale=0.02 * 0.02)
         make_identity(nc, ident[:])
+        fields = {}
+        for f, t in ((0, 0), (1, 0), (0, 1), (1, 1)):
+            fields[f, t] = keep.tile([P, 2 * S], F32, name="field%d%d" % (f, t))
+            nc.vector.memset(fields[f, t][:, S : 2 * S], 0.0)
 
         scales_picked = keep.tile([P, S], U8, name="scales_picked", align_bytes=64)
         nc.vector.tensor_copy(scales_picked[:], scales_all[:].indirect(lists["offs"][:]))
-        words_picked = []
+        words_picked = keep.tile([P, S], U32, name="words_picked", align_bytes=64)
         for h in range(2):
-            wp = keep.tile([P, HALF], U32, name="words_picked%d" % h, align_bytes=64)
-            nc.vector.tensor_copy(wp[:], words_all[:].indirect(lists["offs"][:, h * 16 : (h + 1) * 16]))
-            words_picked.append(wp)
+            nc.vector.tensor_copy(
+                words_picked[:, h * HALF : (h + 1) * HALF],
+                words_all[:].indirect(lists["offs"][:, h * 16 : (h + 1) * 16]),
+            )
 
         codes = {}
         planes = {}
-        fields = {}
-        for f, t in ((0, 0), (0, 1), (1, 0), (1, 1)):
+        def weights(f, t):
             grouped = keep.tile([P, P, PACK], BF16, name="grouped%d%d" % (f, t), align_bytes=64)
-            src = w_raw[f][:, :, t * P : (t + 1) * P].rearrange("p j (c i) -> p c j i", i=4)
+            src = w_raw[f, t].rearrange("p j (c i) -> p c j i", i=4)
             dst = grouped[:].rearrange("p (c i) j -> p c j i", i=4)
-            if f == 0:
+            if t == 0:
                 nc.scalar.copy(dst, src)
             else:
                 nc.vector.tensor_copy(dst, src)
@@ -90,97 +95,156 @@ def tile_picked_yturbo_prod_p_kernel(
                 in_=grouped[:].rearrange("p c j -> p (c j)"),
             )
 
-        for n, (f, t) in enumerate(((0, 0), (1, 0), (0, 1), (1, 1))):
-            fields[f, t] = keep.tile([P, S], F32, name="field%d%d" % (f, t))
-            for h in range(2):
-                bank = psum.tile([P, HALF], F32, name="mm%d%d%d" % (f, t, h), tag="bank%d" % ((2 * n + h) % 4))
-                nc.tensor.matmul_mx(
-                    out=bank[:],
-                    lhsT=codes[f, t][:].bitcast(FP8X4),
-                    lhsT_scale=planes[f, t][:],
-                    rhs=words_picked[h][:].bitcast(FP8X4),
-                    rhs_scale=scales_picked[:, h * HALF : (h + 1) * HALF],
-                    start=True,
-                    stop=True,
-                )
-                if h == 0:
-                    nc.scalar.copy(fields[f, t][:, h * HALF : (h + 1) * HALF], bank[:])
-                else:
-                    nc.vector.tensor_copy(fields[f, t][:, h * HALF : (h + 1) * HALF], bank[:])
+        for f, t in ((0, 0), (1, 0), (1, 1)):
+            weights(f, t)
 
-        state = {}
-
-        def differences(k):
-            t, j0, j1 = PIECES[k]
-            w = j1 - j0
-            u, v = fields[0, t], fields[1, t]
-
-            def at(field, name):
-                return field[:].indirect(lists[name][:, j0 // 16 : j1 // 16])
-
-            def fresh(name):
-                return work.tile([P, w], F32, name=name, tag=name)
-
-            u_s, u_w, v_s = fresh("u_s"), fresh("u_w"), fresh("v_s")
-            nc.scalar.activation(u_s[:], at(u, "south"), ACT.Copy)
-            nc.scalar.activation(u_w[:], at(u, "west"), ACT.Copy)
-            nc.scalar.activation(v_s[:], at(v, "south"), ACT.Copy)
-            a, b, c, x, p, q = (fresh(name) for name in ("a", "b", "c", "x", "p", "q"))
-            nc.vector.tensor_tensor(c[:], at(u, "north"), u_s[:], ALU.subtract)
-            nc.vector.tensor_tensor(a[:], at(u, "east"), u_w[:], ALU.subtract)
-            nc.vector.tensor_tensor(x[:], at(v, "west"), c[:], ALU.subtract)
-            nc.vector.tensor_tensor(b[:], at(v, "north"), v_s[:], ALU.subtract)
-            nc.vector.tensor_tensor(p[:], at(v, "east"), x[:], ALU.subtract)
-            nc.vector.scalar_tensor_tensor(q[:], c[:], 2.0, p[:], ALU.mult, ALU.subtract)
-            state[k] = (a, b, p, q)
-
-        def squares(k):
-            t, j0, j1 = PIECES[k]
-            w = j1 - j0
-            a, b, p, q = state[k]
-            sq = [work.tile([P, w], F32, name="sq%d" % i, tag="sq%d" % i) for i in range(4)]
-            nc.scalar.activation(sq[0][:], a[:], ACT.Square, scale=math.sqrt(0.5))
-            nc.scalar.activation(sq[1][:], b[:], ACT.Square, scale=math.sqrt(0.5))
-            nc.scalar.activation(sq[2][:], p[:], ACT.Square, scale=0.5)
-            nc.scalar.activation(sq[3][:], q[:], ACT.Square, scale=math.sqrt(0.05))
-            strain = psum.tile([P, w], F32, name="strain%d" % k, tag="strain%d" % (k % 2))
-            for blk in range(w // P):
-                cols = slice(blk * P, (blk + 1) * P)
-                terms = [floor_col[:].to_broadcast([P, P])] + [s[:, cols] for s in sq[:3]]
-                for i, term in enumerate(terms):
-                    nc.tensor.matmul(
-                        strain[:, cols], lhsT=term, rhs=ident[:], is_transpose=True, start=(i == 0), stop=(i == 3)
-                    )
-            state[k] = (strain, sq[3])
-
-        def finish(k):
-            t, j0, j1 = PIECES[k]
-            w = j1 - j0
-            strain, rot2 = state[k]
-            smag = work.tile([P, w], F32, name="smag", tag="smag")
-            nc.scalar.activation(smag[:], strain[:], ACT.Sqrt)
-            cube = work.tile([P, w], F32, name="cube", tag="cube")
-            back = psum.tile([P, w], F32, name="back%d" % k, tag="back%d" % (k % 2))
-            for blk in range(w // P):
-                cols = slice(blk * P, (blk + 1) * P)
-                jb = j0 // P + blk
-                nc.vector.scalar_tensor_tensor(
-                    cube[:, cols], strain[:, cols], wall_cols[:, jb : jb + 1], smag[:, cols], ALU.mult, ALU.mult
-                )
-            for blk in range(w // P):
-                cols = slice(blk * P, (blk + 1) * P)
-                nc.tensor.transpose(back[:, cols], cube[:, cols], ident[:])
-            result = work.tile([P, w], F32, name="result", tag="result")
-            nc.vector.scalar_tensor_tensor(
-                result[:], back[:], csd_cols[:, t : t + 1], rot2[:], ALU.mult, ALU.subtract
+        def product(f, t, cols, tag):
+            bank = psum.tile([P, cols.stop - cols.start], F32, name="mm%d%d%d" % (f, t, cols.start), tag=tag)
+            nc.tensor.matmul_mx(
+                out=bank[:],
+                lhsT=codes[f, t][:].bitcast(FP8X4),
+                lhsT_scale=planes[f, t][:],
+                rhs=words_picked[:, cols].bitcast(FP8X4),
+                rhs_scale=scales_picked[:, cols],
+                start=True,
+                stop=True,
             )
-            nc.sync.dma_start(out[t * P : (t + 1) * P, j0:j1], result[:])
+            return bank
 
-        count = len(PIECES)
-        for step in range(count + 2):
-            if step < count:
-                differences(step)
-            if 0 <= step - 1 < count:
-                squares(step - 1)
-            if 0 <= step - 2 < count:
-                finish(step - 2)
+        nc.scalar.copy(fields[0, 0][:, 0:HALF], product(0, 0, slice(0, HALF), "bank0")[:])
+        nc.vector.tensor_copy(fields[0, 0][:, HALF:S], product(0, 0, slice(HALF, S), "bank1")[:])
+        bank_v0 = product(1, 0, slice(0, S), "bank2")
+
+        WHOLE = slice(0, S)
+        HALVES = [slice(0, HALF), slice(HALF, S)]
+        tiles = {}
+
+        def tile(name, t):
+            if (name, t) not in tiles:
+                tag = {("cube", 0): "p1", ("q2", 1): "smag0"}.get((name, t), "%s%d" % (name, t))
+                tiles[name, t] = keep.tile([P, S], F32, name="%s%d" % (name, t), tag=tag)
+            return tiles[name, t]
+
+        def at(f, t, name, cols):
+            return fields[f, t][:].indirect(lists[name][:, cols.start // 16 : cols.stop // 16])
+
+        def fetch(engine, dst, f, t, name, cols):
+            if engine == "scalar":
+                nc.scalar.activation(tile(dst, t)[:, cols], at(f, t, name, cols), ACT.Copy)
+            else:
+                nc.vector.tensor_copy(tile(dst, t)[:, cols], at(f, t, name, cols))
+
+        def fetch_less(dst, f, t, name, other, cols):
+            nc.vector.tensor_tensor(tile(dst, t)[:, cols], at(f, t, name, cols), tile(other, t)[:, cols], ALU.subtract)
+
+        def square(name, t, cols, factor):
+            nc.scalar.activation(
+                tile(name + "2", t)[:, cols], tile(name, t)[:, cols], ACT.Square, scale=math.sqrt(factor)
+            )
+
+        strain = {}
+
+        def strain_passes(t, h, names, first, last):
+            if first:
+                strain[t, h] = psum.tile([P, HALF], F32, name="strain%d%d" % (t, h), tag="bank%d" % (4 + 2 * t + h))
+            passes = []
+            for name in names:
+                for c0 in range(0, HALF, P):
+                    if name == "floor":
+                        term = floor_col[:].to_broadcast([P, P])
+                    else:
+                        term = tile(name, t)[:, h * HALF + c0 : h * HALF + c0 + P]
+                    passes.append((c0, term))
+            for i, (c0, term) in enumerate(passes):
+                nc.tensor.matmul(
+                    strain[t, h][:, c0 : c0 + P],
+                    lhsT=term,
+                    rhs=ident[:],
+                    is_transpose=True,
+                    start=(first and i == 0),
+                    stop=(last and i == len(passes) - 1),
+                )
+
+        def root(t, h):
+            nc.scalar.activation(tile("smag", t)[:, HALVES[h]], strain[t, h][:], ACT.Sqrt)
+
+        backs = {}
+
+        def cube(t, h):
+            made = tile("cube", t)[:, HALVES[h]]
+            backs[t, h] = psum.tile([P, HALF], F32, name="back%d%d" % (t, h), tag="bank%d" % (2 * t + h))
+            for c0 in range(0, HALF, P):
+                j0 = h * HALF + c0
+                nc.vector.scalar_tensor_tensor(
+                    made[:, c0 : c0 + P],
+                    strain[t, h][:, c0 : c0 + P],
+                    wall_cols[:, j0 // P : j0 // P + 1],
+                    tile("smag", t)[:, j0 : j0 + P],
+                    ALU.mult,
+                    ALU.mult,
+                )
+            for c0 in range(0, HALF, P):
+                nc.tensor.transpose(backs[t, h][:, c0 : c0 + P], made[:, c0 : c0 + P], ident[:])
+
+        def result(t, h):
+            cols = HALVES[h]
+            nc.vector.scalar_tensor_tensor(
+                tile("result", t)[:, cols],
+                backs[t, h][:],
+                csd_cols[:, t : t + 1],
+                tile("q2", t)[:, cols],
+                ALU.mult,
+                ALU.subtract,
+            )
+            nc.sync.dma_start(out[t * P : (t + 1) * P, cols], tile("result", t)[:, cols])
+
+        fetch("scalar", "u_s", 0, 0, "south", WHOLE)
+        fetch("vector", "u_w", 0, 0, "west", WHOLE)
+        weights(0, 1)
+        late = [(1, 1, product(1, 1, WHOLE, "bank3")), (0, 1, product(0, 1, WHOLE, "bank0"))]
+        nc.scalar.copy(fields[1, 0][:, 0:S], bank_v0[:])
+        fetch("scalar", "v_w", 1, 0, "west", WHOLE)
+        fetch("scalar", "v_s", 1, 0, "south", WHOLE)
+        fetch_less("c", 0, 0, "north", "u_s", WHOLE)
+        fetch_less("a", 0, 0, "east", "u_w", WHOLE)
+        fetch_less("d", 1, 0, "east", "v_w", WHOLE)
+        fetch_less("b", 1, 0, "north", "v_s", WHOLE)
+        nc.vector.tensor_tensor(tile("p", 0)[:], tile("c", 0)[:], tile("d", 0)[:], ALU.add)
+        nc.vector.tensor_tensor(tile("q", 0)[:], tile("c", 0)[:], tile("d", 0)[:], ALU.subtract)
+        for f, t, bank in late:
+            nc.scalar.copy(fields[f, t][:, 0:S], bank[:])
+        fetch("scalar", "v_s", 1, 1, "south", WHOLE)
+        fetch("scalar", "u_s", 0, 1, "south", WHOLE)
+        fetch("scalar", "u_w", 0, 1, "west", WHOLE)
+        for name, factor in (("a", 0.5), ("b", 0.5), ("p", 0.25)):
+            square(name, 0, WHOLE, factor)
+        for h in range(2):
+            strain_passes(0, h, ("floor", "a2", "b2", "p2"), True, True)
+            root(0, h)
+        square("q", 0, WHOLE, 0.05)
+        fetch_less("b", 1, 1, "north", "v_s", WHOLE)
+        fetch_less("c", 0, 1, "north", "u_s", WHOLE)
+        fetch_less("a", 0, 1, "east", "u_w", WHOLE)
+        for cols in HALVES:
+            fetch_less("x", 1, 1, "west", "c", cols)
+        square("b", 1, WHOLE, 0.5)
+        square("a", 1, WHOLE, 0.5)
+        for h in range(2):
+            strain_passes(1, h, ("floor", "b2", "a2"), True, False)
+        for h in range(2):
+            fetch_less("p", 1, 1, "east", "x", HALVES[h])
+            square("p", 1, HALVES[h], 0.25)
+            strain_passes(1, h, ("p2",), False, True)
+            root(1, h)
+        for cols in HALVES:
+            nc.vector.scalar_tensor_tensor(
+                tile("q", 1)[:, cols], tile("c", 1)[:, cols], 2.0, tile("p", 1)[:, cols], ALU.mult, ALU.subtract
+            )
+        cube(0, 0)
+        cube(0, 1)
+        square("q", 1, WHOLE, 0.05)
+        cube(1, 0)
+        cube(1, 1)
+        for t in range(2):
+            for h in range(2):
+                result(t, h)

@@ -51,11 +51,11 @@ def tile_picked_yturbo_prod_p_kernel(
             nc.sync.dma_start(
                 scales_all[32 * q : 32 * q + 4, :].bitcast(I32), x_scales[0, 4 * q : 4 * q + 4, :].bitcast(I32)
             )
-        nc.sync.dma_start(words_all[:].bitcast(I32), x_words[0].rearrange("p n t -> p (n t)").bitcast(I32))
         nc.sync.dma_start(w1_raw[0][:], w1[:, 0:P].rearrange("(p j) n -> p j n", j=PACK))
+        nc.sync.dma_start(words_all[:].bitcast(I32), x_words[0].rearrange("p n t -> p (n t)").bitcast(I32))
         nc.sync.dma_start(w2_raw[:], w2.rearrange("(p j) n -> p j n", j=PACK))
-        nc.sync.dma_start(lists["west"][:], west)
         nc.sync.dma_start(w1_raw[1][:], w1[:, P:N].rearrange("(p j) n -> p j n", j=PACK))
+        nc.sync.dma_start(lists["west"][:], west)
         nc.sync.dma_start(lists["north"][:], north)
         nc.sync.dma_start(lists["east"][:], east)
         with nc.allow_non_contiguous_dma(reason="one factor a partition"):
@@ -66,24 +66,17 @@ def tile_picked_yturbo_prod_p_kernel(
         fields = {}
         for f, t in ((0, 0), (1, 0), (0, 1), (1, 1)):
             fields[f, t] = keep.tile([P, 2 * S], F32, name="field%d%d" % (f, t))
-            nc.vector.memset(fields[f, t][:, S : 2 * S], 0.0)
+            nc.vector.memset(fields[f, t][:, S : 2 * S].bitcast(I32), 0)
 
         scales_picked = keep.tile([P, S], U8, name="scales_picked", align_bytes=64)
         nc.vector.tensor_copy(scales_picked[:], scales_all[:].indirect(lists["offs"][:]))
-        words_picked = keep.tile([P, S], U32, name="words_picked", align_bytes=64)
-        for h in range(2):
-            nc.vector.tensor_copy(
-                words_picked[:, h * HALF : (h + 1) * HALF],
-                words_all[:].indirect(lists["offs"][:, h * 16 : (h + 1) * 16]),
-            )
-
         codes = {}
         planes = {}
         def weights(f, t):
-            grouped = keep.tile([P, P, PACK], BF16, name="grouped%d%d" % (f, t), align_bytes=64)
+            grouped = keep.tile([P, P, PACK], BF16, name="grouped%d%d" % (f, t), tag="grouped%d" % (t if f else 0), align_bytes=64)
             src = w_raw[f, t].rearrange("p j (c i) -> p c j i", i=4)
             dst = grouped[:].rearrange("p (c i) j -> p c j i", i=4)
-            if t == 0:
+            if (f, t) == (0, 0):
                 nc.scalar.copy(dst, src)
             else:
                 nc.vector.tensor_copy(dst, src)
@@ -95,7 +88,14 @@ def tile_picked_yturbo_prod_p_kernel(
                 in_=grouped[:].rearrange("p c j -> p (c j)"),
             )
 
-        for f, t in ((0, 0), (1, 0), (1, 1)):
+        weights(0, 0)
+        words_picked = keep.tile([P, S], U32, name="words_picked", align_bytes=64)
+        first_cols = [slice(0, 256), slice(256, 384), slice(384, 512)]
+        for cols in first_cols:
+            nc.vector.tensor_copy(
+                words_picked[:, cols], words_all[:].indirect(lists["offs"][:, cols.start // 16 : cols.stop // 16])
+            )
+        for f, t in ((1, 0), (1, 1), (0, 1)):
             weights(f, t)
 
         def product(f, t, cols, tag):
@@ -111,9 +111,9 @@ def tile_picked_yturbo_prod_p_kernel(
             )
             return bank
 
-        nc.scalar.copy(fields[0, 0][:, 0:HALF], product(0, 0, slice(0, HALF), "bank0")[:])
-        nc.vector.tensor_copy(fields[0, 0][:, HALF:S], product(0, 0, slice(HALF, S), "bank1")[:])
-        bank_v0 = product(1, 0, slice(0, S), "bank2")
+        for i, cols in enumerate(first_cols):
+            nc.scalar.copy(fields[0, 0][:, cols], product(0, 0, cols, "bank%d" % i)[:])
+        bank_v0 = product(1, 0, slice(0, S), "bank3")
 
         WHOLE = slice(0, S)
         HALVES = [slice(0, HALF), slice(HALF, S)]
@@ -200,8 +200,7 @@ def tile_picked_yturbo_prod_p_kernel(
 
         fetch("scalar", "u_s", 0, 0, "south", WHOLE)
         fetch("vector", "u_w", 0, 0, "west", WHOLE)
-        weights(0, 1)
-        late = [(1, 1, product(1, 1, WHOLE, "bank3")), (0, 1, product(0, 1, WHOLE, "bank0"))]
+        late = [(1, 1, product(1, 1, WHOLE, "bank0")), (0, 1, product(0, 1, WHOLE, "bank1"))]
         nc.scalar.copy(fields[1, 0][:, 0:S], bank_v0[:])
         fetch("scalar", "v_w", 1, 0, "west", WHOLE)
         fetch("scalar", "v_s", 1, 0, "south", WHOLE)

@@ -17,8 +17,16 @@ ALU = mybir.AluOpType
 P = 128
 K, T, S, N = 512, 1024, 512, 256
 PACK = 4
+GROUP = 16
 HALF = S // 2
 FLOPS = 2 * 2 * K * N * S
+
+UU, VV = 0, 1
+FLOOR = 0.02
+WHOLE = slice(0, S)
+HALVES = [slice(0, HALF), slice(HALF, S)]
+FIRST_PIECES = [slice(0, 256), slice(256, 384), slice(384, 512)]
+REUSES = {("cube", 0): "p1", ("q2", 0): "v_w1", ("q2", 1): "smag0"}
 
 
 def tile_picked_yturbo_prod_p_kernel(
@@ -31,12 +39,12 @@ def tile_picked_yturbo_prod_p_kernel(
 
         lists = {}
         for name in ("offs", "east", "west", "north", "south"):
-            lists[name] = keep.tile([P, S // 16], U16, name="list_" + name)
+            lists[name] = keep.tile([P, S // GROUP], U16, name="list_" + name)
         words_all = keep.tile([P, T], U32, name="words_all", align_bytes=64)
         scales_all = keep.tile([P, T], U8, name="scales_all", align_bytes=64)
         w1_raw = [keep.tile([P, PACK, P], F32, name="w1_raw%d" % t) for t in range(2)]
         w2_raw = keep.tile([P, PACK, N], F32, name="w2_raw")
-        w_raw = {(0, 0): w1_raw[0][:], (0, 1): w1_raw[1][:], (1, 0): w2_raw[:, :, 0:P], (1, 1): w2_raw[:, :, P:N]}
+        w_raw = {(UU, 0): w1_raw[0][:], (UU, 1): w1_raw[1][:], (VV, 0): w2_raw[:, :, 0:P], (VV, 1): w2_raw[:, :, P:N]}
         one = keep.tile([P, 1], F32, name="one")
         floor_col = keep.tile([P, 1], F32, name="floor_col")
         wall_cols = keep.tile([P, S // P], F32, name="wall_cols")
@@ -47,9 +55,10 @@ def tile_picked_yturbo_prod_p_kernel(
         nc.vector.memset(one[:], 1.0)
         nc.sync.dma_start(lists["offs"][:], offs)
         nc.sync.dma_start(lists["south"][:], south)
-        for q in range(4):
+        for quadrant in range(4):
             nc.sync.dma_start(
-                scales_all[32 * q : 32 * q + 4, :].bitcast(I32), x_scales[0, 4 * q : 4 * q + 4, :].bitcast(I32)
+                scales_all[32 * quadrant : 32 * quadrant + 4, :].bitcast(I32),
+                x_scales[0, 4 * quadrant : 4 * quadrant + 4, :].bitcast(I32),
             )
         nc.sync.dma_start(w1_raw[0][:], w1[:, 0:P].rearrange("(p j) n -> p j n", j=PACK))
         nc.sync.dma_start(words_all[:].bitcast(I32), x_words[0].rearrange("p n t -> p (n t)").bitcast(I32))
@@ -59,92 +68,87 @@ def tile_picked_yturbo_prod_p_kernel(
         nc.sync.dma_start(lists["north"][:], north)
         nc.sync.dma_start(lists["east"][:], east)
         with nc.allow_non_contiguous_dma(reason="one factor a partition"):
-            nc.sync.dma_start(wall_cols[:], wall[0:1, :].rearrange("o (b p) -> p (o b)", p=P))
+            nc.sync.dma_start(wall_cols[:], wall[0:1, :].rearrange("o (i p) -> p (o i)", p=P))
             nc.sync.dma_start(csd_cols[:], csd.rearrange("(t p) o -> p (t o)", p=P))
-        nc.scalar.activation(floor_col[:], one[:], ACT.Sqrt, scale=0.02 * 0.02)
+        nc.scalar.activation(floor_col[:], one[:], ACT.Sqrt, scale=FLOOR * FLOOR)
         make_identity(nc, ident[:])
+
         fields = {}
-        for f, t in ((0, 0), (1, 0), (0, 1), (1, 1)):
+        for f, t in ((UU, 0), (VV, 0), (UU, 1), (VV, 1)):
             fields[f, t] = keep.tile([P, 2 * S], F32, name="field%d%d" % (f, t))
             nc.vector.memset(fields[f, t][:, S : 2 * S].bitcast(I32), 0)
 
+        def entries(name, cols):
+            return lists[name][:, cols.start // GROUP : cols.stop // GROUP]
+
         scales_picked = keep.tile([P, S], U8, name="scales_picked", align_bytes=64)
         nc.vector.tensor_copy(scales_picked[:], scales_all[:].indirect(lists["offs"][:]))
+
         codes = {}
-        planes = {}
-        def weights(f, t):
-            grouped = keep.tile([P, P, PACK], BF16, name="grouped%d%d" % (f, t), tag="grouped%d" % (t if f else 0), align_bytes=64)
-            src = w_raw[f, t].rearrange("p j (c i) -> p c j i", i=4)
-            dst = grouped[:].rearrange("p (c i) j -> p c j i", i=4)
-            if (f, t) == (0, 0):
-                nc.scalar.copy(dst, src)
-            else:
-                nc.vector.tensor_copy(dst, src)
+        code_scales = {}
+
+        def quantise_weights(f, t, cast, staging):
+            grouped = keep.tile([P, P, PACK], BF16, name="grouped%d%d" % (f, t), tag=staging, align_bytes=64)
+            cast(
+                grouped[:].rearrange("p (c i) j -> p c j i", i=4),
+                w_raw[f, t].rearrange("p j (c i) -> p c j i", i=4),
+            )
             codes[f, t] = keep.tile([P, P], U32, name="codes%d%d" % (f, t), align_bytes=64)
-            planes[f, t] = keep.tile([P, P], U8, name="planes%d%d" % (f, t), align_bytes=64)
+            code_scales[f, t] = keep.tile([P, P], U8, name="code_scales%d%d" % (f, t), align_bytes=64)
             nc.vector.quantize_mx(
                 out=codes[f, t][:].bitcast(FP8X4),
-                scales=planes[f, t][:],
+                scales=code_scales[f, t][:],
                 in_=grouped[:].rearrange("p c j -> p (c j)"),
             )
 
-        weights(0, 0)
+        quantise_weights(UU, 0, nc.scalar.copy, "staging0")
         words_picked = keep.tile([P, S], U32, name="words_picked", align_bytes=64)
-        first_cols = [slice(0, 256), slice(256, 384), slice(384, 512)]
-        for cols in first_cols:
-            nc.vector.tensor_copy(
-                words_picked[:, cols], words_all[:].indirect(lists["offs"][:, cols.start // 16 : cols.stop // 16])
-            )
-        for f, t in ((1, 0), (1, 1), (0, 1)):
-            weights(f, t)
+        for cols in FIRST_PIECES:
+            nc.vector.tensor_copy(words_picked[:, cols], words_all[:].indirect(entries("offs", cols)))
+        quantise_weights(VV, 0, nc.vector.tensor_copy, "staging0")
+        quantise_weights(VV, 1, nc.vector.tensor_copy, "staging1")
+        quantise_weights(UU, 1, nc.vector.tensor_copy, "staging0")
 
-        def product(f, t, cols, tag):
-            bank = psum.tile([P, cols.stop - cols.start], F32, name="mm%d%d%d" % (f, t, cols.start), tag=tag)
+        def product(f, t, cols, bank):
+            acc = psum.tile([P, cols.stop - cols.start], F32, name="acc%d%d%d" % (f, t, bank), tag="bank%d" % bank)
             nc.tensor.matmul_mx(
-                out=bank[:],
+                out=acc[:],
                 lhsT=codes[f, t][:].bitcast(FP8X4),
-                lhsT_scale=planes[f, t][:],
+                lhsT_scale=code_scales[f, t][:],
                 rhs=words_picked[:, cols].bitcast(FP8X4),
                 rhs_scale=scales_picked[:, cols],
                 start=True,
                 stop=True,
             )
-            return bank
+            return acc
 
-        for i, cols in enumerate(first_cols):
-            nc.scalar.copy(fields[0, 0][:, cols], product(0, 0, cols, "bank%d" % i)[:])
-        bank_v0 = product(1, 0, slice(0, S), "bank3")
+        work_tiles = {}
 
-        WHOLE = slice(0, S)
-        HALVES = [slice(0, HALF), slice(HALF, S)]
-        tiles = {}
+        def work(name, t):
+            if (name, t) not in work_tiles:
+                tag = REUSES.get((name, t), "%s%d" % (name, t))
+                work_tiles[name, t] = keep.tile([P, S], F32, name="%s%d" % (name, t), tag=tag)
+            return work_tiles[name, t]
 
-        def tile(name, t):
-            if (name, t) not in tiles:
-                tag = {("cube", 0): "p1", ("q2", 1): "smag0"}.get((name, t), "%s%d" % (name, t))
-                tiles[name, t] = keep.tile([P, S], F32, name="%s%d" % (name, t), tag=tag)
-            return tiles[name, t]
+        def gathered(f, t, name, cols):
+            return fields[f, t][:].indirect(entries(name, cols))
 
-        def at(f, t, name, cols):
-            return fields[f, t][:].indirect(lists[name][:, cols.start // 16 : cols.stop // 16])
+        def fetch(dst, f, t, name, cols):
+            nc.scalar.activation(work(dst, t)[:, cols], gathered(f, t, name, cols), ACT.Copy)
 
-        def fetch(engine, dst, f, t, name, cols):
-            if engine == "scalar":
-                nc.scalar.activation(tile(dst, t)[:, cols], at(f, t, name, cols), ACT.Copy)
-            else:
-                nc.vector.tensor_copy(tile(dst, t)[:, cols], at(f, t, name, cols))
-
-        def fetch_less(dst, f, t, name, other, cols):
-            nc.vector.tensor_tensor(tile(dst, t)[:, cols], at(f, t, name, cols), tile(other, t)[:, cols], ALU.subtract)
+        def fetch_minus(dst, f, t, name, other, cols):
+            nc.vector.tensor_tensor(
+                work(dst, t)[:, cols], gathered(f, t, name, cols), work(other, t)[:, cols], ALU.subtract
+            )
 
         def square(name, t, cols, factor):
             nc.scalar.activation(
-                tile(name + "2", t)[:, cols], tile(name, t)[:, cols], ACT.Square, scale=math.sqrt(factor)
+                work(name + "2", t)[:, cols], work(name, t)[:, cols], ACT.Square, scale=math.sqrt(factor)
             )
 
         strain = {}
 
-        def strain_passes(t, h, names, first, last):
+        def add_to_strain(t, h, names, first, last):
             if first:
                 strain[t, h] = psum.tile([P, HALF], F32, name="strain%d%d" % (t, h), tag="bank%d" % (4 + 2 * t + h))
             passes = []
@@ -153,7 +157,7 @@ def tile_picked_yturbo_prod_p_kernel(
                     if name == "floor":
                         term = floor_col[:].to_broadcast([P, P])
                     else:
-                        term = tile(name, t)[:, h * HALF + c0 : h * HALF + c0 + P]
+                        term = work(name, t)[:, h * HALF + c0 : h * HALF + c0 + P]
                     passes.append((c0, term))
             for i, (c0, term) in enumerate(passes):
                 nc.tensor.matmul(
@@ -166,84 +170,91 @@ def tile_picked_yturbo_prod_p_kernel(
                 )
 
         def root(t, h):
-            nc.scalar.activation(tile("smag", t)[:, HALVES[h]], strain[t, h][:], ACT.Sqrt)
+            nc.scalar.activation(work("smag", t)[:, HALVES[h]], strain[t, h][:], ACT.Sqrt)
 
-        backs = {}
+        cube_back = {}
 
         def cube(t, h):
-            made = tile("cube", t)[:, HALVES[h]]
-            backs[t, h] = psum.tile([P, HALF], F32, name="back%d%d" % (t, h), tag="bank%d" % (2 * t + h))
+            made = work("cube", t)
+            cube_back[t, h] = psum.tile([P, HALF], F32, name="back%d%d" % (t, h), tag="bank%d" % (2 * t + h))
             for c0 in range(0, HALF, P):
                 j0 = h * HALF + c0
                 nc.vector.scalar_tensor_tensor(
-                    made[:, c0 : c0 + P],
+                    made[:, j0 : j0 + P],
                     strain[t, h][:, c0 : c0 + P],
                     wall_cols[:, j0 // P : j0 // P + 1],
-                    tile("smag", t)[:, j0 : j0 + P],
+                    work("smag", t)[:, j0 : j0 + P],
                     ALU.mult,
                     ALU.mult,
                 )
             for c0 in range(0, HALF, P):
-                nc.tensor.transpose(backs[t, h][:, c0 : c0 + P], made[:, c0 : c0 + P], ident[:])
+                j0 = h * HALF + c0
+                nc.tensor.transpose(cube_back[t, h][:, c0 : c0 + P], made[:, j0 : j0 + P], ident[:])
 
         def result(t, h):
             cols = HALVES[h]
             nc.vector.scalar_tensor_tensor(
-                tile("result", t)[:, cols],
-                backs[t, h][:],
+                work("result", t)[:, cols],
+                cube_back[t, h][:],
                 csd_cols[:, t : t + 1],
-                tile("q2", t)[:, cols],
+                work("q2", t)[:, cols],
                 ALU.mult,
                 ALU.subtract,
             )
-            nc.sync.dma_start(out[t * P : (t + 1) * P, cols], tile("result", t)[:, cols])
+            nc.sync.dma_start(out[t * P : (t + 1) * P, cols], work("result", t)[:, cols])
 
-        fetch("scalar", "u_s", 0, 0, "south", WHOLE)
-        fetch("vector", "u_w", 0, 0, "west", WHOLE)
-        late = [(1, 1, product(1, 1, WHOLE, "bank0")), (0, 1, product(0, 1, WHOLE, "bank1"))]
-        nc.scalar.copy(fields[1, 0][:, 0:S], bank_v0[:])
-        fetch("scalar", "v_w", 1, 0, "west", WHOLE)
-        fetch("scalar", "v_s", 1, 0, "south", WHOLE)
-        fetch_less("c", 0, 0, "north", "u_s", WHOLE)
-        fetch_less("a", 0, 0, "east", "u_w", WHOLE)
-        fetch_less("d", 1, 0, "east", "v_w", WHOLE)
-        fetch_less("b", 1, 0, "north", "v_s", WHOLE)
-        nc.vector.tensor_tensor(tile("p", 0)[:], tile("c", 0)[:], tile("d", 0)[:], ALU.add)
-        nc.vector.tensor_tensor(tile("q", 0)[:], tile("c", 0)[:], tile("d", 0)[:], ALU.subtract)
-        for f, t, bank in late:
-            nc.scalar.copy(fields[f, t][:, 0:S], bank[:])
-        fetch("scalar", "v_s", 1, 1, "south", WHOLE)
-        fetch("scalar", "u_s", 0, 1, "south", WHOLE)
-        fetch("scalar", "u_w", 0, 1, "west", WHOLE)
+        for bank, cols in enumerate(FIRST_PIECES):
+            nc.scalar.copy(fields[UU, 0][:, cols], product(UU, 0, cols, bank)[:])
+        acc_v0 = product(VV, 0, WHOLE, 3)
+        for cols in HALVES:
+            fetch("u_s", UU, 0, "south", cols)
+        nc.vector.tensor_copy(work("u_w", 0)[:, HALVES[0]], gathered(UU, 0, "west", HALVES[0]))
+        fetch("u_w", UU, 0, "west", HALVES[1])
+        acc_v1 = product(VV, 1, WHOLE, 0)
+        acc_u1 = product(UU, 1, WHOLE, 1)
+        nc.scalar.copy(fields[VV, 0][:, WHOLE], acc_v0[:])
+        fetch("v_s", VV, 0, "south", WHOLE)
+        for cols in HALVES:
+            fetch_minus("c", UU, 0, "north", "u_s", cols)
+            fetch_minus("a", UU, 0, "east", "u_w", cols)
+        fetch_minus("x", VV, 0, "west", "c", WHOLE)
+        fetch_minus("b", VV, 0, "north", "v_s", WHOLE)
+        fetch_minus("p", VV, 0, "east", "x", WHOLE)
+
+        nc.scalar.copy(fields[VV, 1][:, WHOLE], acc_v1[:])
+        nc.scalar.copy(fields[UU, 1][:, WHOLE], acc_u1[:])
+        fetch("v_s", VV, 1, "south", WHOLE)
+        fetch("u_s", UU, 1, "south", WHOLE)
+        fetch("u_w", UU, 1, "west", WHOLE)
+        fetch("v_w", VV, 1, "west", WHOLE)
         for name, factor in (("a", 0.5), ("b", 0.5), ("p", 0.25)):
             square(name, 0, WHOLE, factor)
         for h in range(2):
-            strain_passes(0, h, ("floor", "a2", "b2", "p2"), True, True)
+            add_to_strain(0, h, ("floor", "a2", "b2", "p2"), True, True)
             root(0, h)
-        square("q", 0, WHOLE, 0.05)
-        fetch_less("b", 1, 1, "north", "v_s", WHOLE)
-        fetch_less("c", 0, 1, "north", "u_s", WHOLE)
-        fetch_less("a", 0, 1, "east", "u_w", WHOLE)
-        for cols in HALVES:
-            fetch_less("x", 1, 1, "west", "c", cols)
+
+        fetch_minus("b", VV, 1, "north", "v_s", WHOLE)
+        nc.vector.scalar_tensor_tensor(work("q", 0)[:], work("c", 0)[:], 2.0, work("p", 0)[:], ALU.mult, ALU.subtract)
+        fetch_minus("c", UU, 1, "north", "u_s", WHOLE)
+        fetch_minus("a", UU, 1, "east", "u_w", WHOLE)
         square("b", 1, WHOLE, 0.5)
         square("a", 1, WHOLE, 0.5)
         for h in range(2):
-            strain_passes(1, h, ("floor", "b2", "a2"), True, False)
-        for h in range(2):
-            fetch_less("p", 1, 1, "east", "x", HALVES[h])
-            square("p", 1, HALVES[h], 0.25)
-            strain_passes(1, h, ("p2",), False, True)
-            root(1, h)
+            add_to_strain(1, h, ("floor", "b2", "a2"), True, False)
         for cols in HALVES:
-            nc.vector.scalar_tensor_tensor(
-                tile("q", 1)[:, cols], tile("c", 1)[:, cols], 2.0, tile("p", 1)[:, cols], ALU.mult, ALU.subtract
-            )
-        cube(0, 0)
-        cube(0, 1)
-        square("q", 1, WHOLE, 0.05)
-        cube(1, 0)
-        cube(1, 1)
+            fetch_minus("d", VV, 1, "east", "v_w", cols)
+        for h, cols in enumerate(HALVES):
+            nc.vector.tensor_tensor(work("p", 1)[:, cols], work("c", 1)[:, cols], work("d", 1)[:, cols], ALU.add)
+            square("p", 1, cols, 0.25)
+            add_to_strain(1, h, ("p2",), False, True)
+            root(1, h)
+        nc.vector.tensor_tensor(work("q", 1)[:], work("c", 1)[:], work("d", 1)[:], ALU.subtract)
+
+        for t in range(2):
+            for cols in HALVES:
+                square("q", t, cols, 0.05)
+            for h in range(2):
+                cube(t, h)
         for t in range(2):
             for h in range(2):
                 result(t, h)

import math
from contextlib import ExitStack

import concourse.mybir as mybir
from concourse.masks import make_identity

F32 = mybir.dt.float32
BF16 = mybir.dt.bfloat16
I32 = mybir.dt.int32
U32 = mybir.dt.uint32
U16 = mybir.dt.uint16
U8 = mybir.dt.uint8
FP8X4 = mybir.dt.float8_e4m3fn_x4
ACT = mybir.ActivationFunctionType
ALU = mybir.AluOpType

P = 128
K, T, S, N = 512, 1024, 512, 256
PACK = 4
GROUP = 16
HALF = S // 2
FLOPS = 2 * 2 * K * N * S

UU, VV = 0, 1
FLOOR = 0.02
WHOLE = slice(0, S)
HALVES = [slice(0, HALF), slice(HALF, S)]
FIRST_PIECES = [slice(0, 256), slice(256, 384), slice(384, 512)]
REUSES = {("cube", 0): "p1", ("q2", 0): "v_w1", ("q2", 1): "smag0"}


def tile_picked_yturbo_prod_p_kernel(
    tc, x_words, x_scales, w1, w2, csd, wall, offs, east, west, north, south, out
):
    nc = tc.nc
    with ExitStack() as ctx:
        keep = ctx.enter_context(tc.tile_pool(name="keep", bufs=1))
        psum = ctx.enter_context(tc.psum_pool(name="psum", bufs=1))

        lists = {}
        for name in ("offs", "east", "west", "north", "south"):
            lists[name] = keep.tile([P, S // GROUP], U16, name="list_" + name)
        words_all = keep.tile([P, T], U32, name="words_all", align_bytes=64)
        scales_all = keep.tile([P, T], U8, name="scales_all", align_bytes=64)
        w1_raw = [keep.tile([P, PACK, P], F32, name="w1_raw%d" % t) for t in range(2)]
        w2_raw = keep.tile([P, PACK, N], F32, name="w2_raw")
        w_raw = {(UU, 0): w1_raw[0][:], (UU, 1): w1_raw[1][:], (VV, 0): w2_raw[:, :, 0:P], (VV, 1): w2_raw[:, :, P:N]}
        one = keep.tile([P, 1], F32, name="one")
        floor_col = keep.tile([P, 1], F32, name="floor_col")
        wall_cols = keep.tile([P, S // P], F32, name="wall_cols")
        csd_cols = keep.tile([P, N // P], F32, name="csd_cols")
        ident = keep.tile([P, P], F32, name="ident")

        nc.gpsimd.memset(scales_all[:].bitcast(I32), 0)
        nc.vector.memset(one[:], 1.0)
        nc.sync.dma_start(lists["offs"][:], offs)
        nc.sync.dma_start(lists["south"][:], south)
        for quadrant in range(4):
            nc.sync.dma_start(
                scales_all[32 * quadrant : 32 * quadrant + 4, :].bitcast(I32),
                x_scales[0, 4 * quadrant : 4 * quadrant + 4, :].bitcast(I32),
            )
        nc.sync.dma_start(w1_raw[0][:], w1[:, 0:P].rearrange("(p j) n -> p j n", j=PACK))
        nc.sync.dma_start(words_all[:].bitcast(I32), x_words[0].rearrange("p n t -> p (n t)").bitcast(I32))
        nc.sync.dma_start(w2_raw[:], w2.rearrange("(p j) n -> p j n", j=PACK))
        nc.sync.dma_start(w1_raw[1][:], w1[:, P:N].rearrange("(p j) n -> p j n", j=PACK))
        nc.sync.dma_start(lists["west"][:], west)
        nc.sync.dma_start(lists["north"][:], north)
        nc.sync.dma_start(lists["east"][:], east)
        with nc.allow_non_contiguous_dma(reason="one factor a partition"):
            nc.sync.dma_start(wall_cols[:], wall[0:1, :].rearrange("o (i p) -> p (o i)", p=P))
            nc.sync.dma_start(csd_cols[:], csd.rearrange("(t p) o -> p (t o)", p=P))
        nc.scalar.activation(floor_col[:], one[:], ACT.Sqrt, scale=FLOOR * FLOOR)
        make_identity(nc, ident[:])

        fields = {}
        for f, t in ((UU, 0), (VV, 0), (UU, 1), (VV, 1)):
            fields[f, t] = keep.tile([P, 2 * S], F32, name="field%d%d" % (f, t))
            nc.vector.memset(fields[f, t][:, S : 2 * S].bitcast(I32), 0)

        def entries(name, cols):
            return lists[name][:, cols.start // GROUP : cols.stop // GROUP]

        scales_picked = keep.tile([P, S], U8, name="scales_picked", align_bytes=64)
        nc.vector.tensor_copy(scales_picked[:], scales_all[:].indirect(lists["offs"][:]))

        codes = {}
        code_scales = {}

        def quantise_weights(f, t, cast, staging):
            grouped = keep.tile([P, P, PACK], BF16, name="grouped%d%d" % (f, t), tag=staging, align_bytes=64)
            cast(
                grouped[:].rearrange("p (c i) j -> p c j i", i=4),
                w_raw[f, t].rearrange("p j (c i) -> p c j i", i=4),
            )
            codes[f, t] = keep.tile([P, P], U32, name="codes%d%d" % (f, t), align_bytes=64)
            code_scales[f, t] = keep.tile([P, P], U8, name="code_scales%d%d" % (f, t), align_bytes=64)
            nc.vector.quantize_mx(
                out=codes[f, t][:].bitcast(FP8X4),
                scales=code_scales[f, t][:],
                in_=grouped[:].rearrange("p c j -> p (c j)"),
            )

        quantise_weights(UU, 0, nc.scalar.copy, "staging0")
        words_picked = keep.tile([P, S], U32, name="words_picked", align_bytes=64)
        for cols in FIRST_PIECES:
            nc.vector.tensor_copy(words_picked[:, cols], words_all[:].indirect(entries("offs", cols)))
        quantise_weights(VV, 0, nc.vector.tensor_copy, "staging0")
        quantise_weights(VV, 1, nc.vector.tensor_copy, "staging1")
        quantise_weights(UU, 1, nc.vector.tensor_copy, "staging0")

        def product(f, t, cols, bank):
            acc = psum.tile([P, cols.stop - cols.start], F32, name="acc%d%d%d" % (f, t, bank), tag="bank%d" % bank)
            nc.tensor.matmul_mx(
                out=acc[:],
                lhsT=codes[f, t][:].bitcast(FP8X4),
                lhsT_scale=code_scales[f, t][:],
                rhs=words_picked[:, cols].bitcast(FP8X4),
                rhs_scale=scales_picked[:, cols],
                start=True,
                stop=True,
            )
            return acc

        work_tiles = {}

        def work(name, t):
            if (name, t) not in work_tiles:
                tag = REUSES.get((name, t), "%s%d" % (name, t))
                work_tiles[name, t] = keep.tile([P, S], F32, name="%s%d" % (name, t), tag=tag)
            return work_tiles[name, t]

        def gathered(f, t, name, cols):
            return fields[f, t][:].indirect(entries(name, cols))

        def fetch(dst, f, t, name, cols):
            nc.scalar.activation(work(dst, t)[:, cols], gathered(f, t, name, cols), ACT.Copy)

        def fetch_minus(dst, f, t, name, other, cols):
            nc.vector.tensor_tensor(
                work(dst, t)[:, cols], gathered(f, t, name, cols), work(other, t)[:, cols], ALU.subtract
            )

        def square(name, t, cols, factor):
            nc.scalar.activation(
                work(name + "2", t)[:, cols], work(name, t)[:, cols], ACT.Square, scale=math.sqrt(factor)
            )

        strain = {}

        def add_to_strain(t, h, names, first, last):
            if first:
                strain[t, h] = psum.tile([P, HALF], F32, name="strain%d%d" % (t, h), tag="bank%d" % (4 + 2 * t + h))
            passes = []
            for name in names:
                for c0 in range(0, HALF, P):
                    if name == "floor":
                        term = floor_col[:].to_broadcast([P, P])
                    else:
                        term = work(name, t)[:, h * HALF + c0 : h * HALF + c0 + P]
                    passes.append((c0, term))
            for i, (c0, term) in enumerate(passes):
                nc.tensor.matmul(
                    strain[t, h][:, c0 : c0 + P],
                    lhsT=term,
                    rhs=ident[:],
                    is_transpose=True,
                    start=(first and i == 0),
                    stop=(last and i == len(passes) - 1),
                )

        def root(t, h):
            nc.scalar.activation(work("smag", t)[:, HALVES[h]], strain[t, h][:], ACT.Sqrt)

        cube_back = {}

        def cube(t, h):
            made = work("cube", t)
            cube_back[t, h] = psum.tile([P, HALF], F32, name="back%d%d" % (t, h), tag="bank%d" % (2 * t + h))
            for c0 in range(0, HALF, P):
                j0 = h * HALF + c0
                nc.vector.scalar_tensor_tensor(
                    made[:, j0 : j0 + P],
                    strain[t, h][:, c0 : c0 + P],
                    wall_cols[:, j0 // P : j0 // P + 1],
                    work("smag", t)[:, j0 : j0 + P],
                    ALU.mult,
                    ALU.mult,
                )
            for c0 in range(0, HALF, P):
                j0 = h * HALF + c0
                nc.tensor.transpose(cube_back[t, h][:, c0 : c0 + P], made[:, j0 : j0 + P], ident[:])

        def result(t, h):
            cols = HALVES[h]
            nc.vector.scalar_tensor_tensor(
                work("result", t)[:, cols],
                cube_back[t, h][:],
                csd_cols[:, t : t + 1],
                work("q2", t)[:, cols],
                ALU.mult,
                ALU.subtract,
            )
            nc.sync.dma_start(out[t * P : (t + 1) * P, cols], work("result", t)[:, cols])

        for bank, cols in enumerate(FIRST_PIECES):
            nc.scalar.copy(fields[UU, 0][:, cols], product(UU, 0, cols, bank)[:])
        acc_v0 = product(VV, 0, WHOLE, 3)
        for cols in HALVES:
            fetch("u_s", UU, 0, "south", cols)
        nc.vector.tensor_copy(work("u_w", 0)[:, HALVES[0]], gathered(UU, 0, "west", HALVES[0]))
        fetch("u_w", UU, 0, "west", HALVES[1])
        acc_v1 = product(VV, 1, WHOLE, 0)
        acc_u1 = product(UU, 1, WHOLE, 1)
        nc.scalar.copy(fields[VV, 0][:, WHOLE], acc_v0[:])
        fetch("v_s", VV, 0, "south", WHOLE)
        for cols in HALVES:
            fetch_minus("c", UU, 0, "north", "u_s", cols)
            fetch_minus("a", UU, 0, "east", "u_w", cols)
        fetch_minus("x", VV, 0, "west", "c", WHOLE)
        fetch_minus("b", VV, 0, "north", "v_s", WHOLE)
        fetch_minus("p", VV, 0, "east", "x", WHOLE)

        nc.scalar.copy(fields[VV, 1][:, WHOLE], acc_v1[:])
        nc.scalar.copy(fields[UU, 1][:, WHOLE], acc_u1[:])
        fetch("v_s", VV, 1, "south", WHOLE)
        fetch("u_s", UU, 1, "south", WHOLE)
        fetch("u_w", UU, 1, "west", WHOLE)
        fetch("v_w", VV, 1, "west", WHOLE)
        for name, factor in (("a", 0.5), ("b", 0.5), ("p", 0.25)):
            square(name, 0, WHOLE, factor)
        for h in range(2):
            add_to_strain(0, h, ("floor", "a2", "b2", "p2"), True, True)
            root(0, h)

        fetch_minus("b", VV, 1, "north", "v_s", WHOLE)
        nc.vector.scalar_tensor_tensor(work("q", 0)[:], work("c", 0)[:], 2.0, work("p", 0)[:], ALU.mult, ALU.subtract)
        fetch_minus("c", UU, 1, "north", "u_s", WHOLE)
        fetch_minus("a", UU, 1, "east", "u_w", WHOLE)
        square("b", 1, WHOLE, 0.5)
        square("a", 1, WHOLE, 0.5)
        for h in range(2):
            add_to_strain(1, h, ("floor", "b2", "a2"), True, False)
        for cols in HALVES:
            fetch_minus("d", VV, 1, "east", "v_w", cols)
        for h, cols in enumerate(HALVES):
            nc.vector.tensor_tensor(work("p", 1)[:, cols], work("c", 1)[:, cols], work("d", 1)[:, cols], ALU.add)
            square("p", 1, cols, 0.25)
            add_to_strain(1, h, ("p2",), False, True)
            root(1, h)
        nc.vector.tensor_tensor(work("q", 1)[:], work("c", 1)[:], work("d", 1)[:], ALU.subtract)

        for t in range(2):
            for cols in HALVES:
                square("q", t, cols, 0.05)
            for h in range(2):
                cube(t, h)
        for t in range(2):
            for h in range(2):
                result(t, h)
